import numpy as np
import ml_dtypes


def mxq(x, axis, fmt="e4m3"):
    dtype, down = {"e4m3": (ml_dtypes.float8_e4m3fn, 7), "e5m2": (ml_dtypes.float8_e5m2, 14)}[fmt]
    v = np.moveaxis(np.asarray(x, np.float32).astype(ml_dtypes.bfloat16).astype(np.float64), axis, -1)
    blocks = v.reshape(v.shape[:-1] + (-1, 32))
    amax = np.abs(blocks).max(-1, keepdims=True)
    byte = np.maximum(np.where(amax > 0, np.frexp(amax)[1] - 1 + 127, 0) - down, 1)
    scale = np.exp2(byte - 127.0)
    codes = (blocks / scale).astype(np.float32).astype(dtype).astype(np.float64)
    return np.moveaxis((codes * scale).reshape(v.shape), -1, axis)


WIDE = False


def mx_kscale(k):
    if not WIDE:
        return np.ones(k)
    levels = np.array([10, -10, 5, -5, 0])
    if k % 512:
        return np.exp2(np.random.permutation(np.resize(levels, k // 32))).repeat(32)
    a = np.empty((k // 512, 16))
    for p in range(k // 512):
        a[p, :8] = np.random.permutation(np.resize(levels, 8))
        for g in range(8):
            far = levels[np.abs(levels - a[p, g]) >= 10]
            a[p, g + 8] = far[np.random.randint(len(far))]
    return np.exp2(a.ravel()).repeat(32)


def f64(x):
    return np.asarray(x).astype(np.float64)


def striped(idx):
    return np.tile(idx.reshape(-1, 16).T, (8, 1)).astype(np.uint16)


def unstriped(offs):
    return offs[:16].T.reshape(-1).astype(np.int64)


def silu(v):
    return v / (1.0 + np.exp(-np.maximum(v, -700.0)))


K, T, E, C, H, N = 512, 1280, 8, 256, 512, 256
TOP = 3
PAD = 64


def by_expert(wq, xq):
    return np.concatenate([wq[e].T @ xq[:, e * C:(e + 1) * C] for e in range(E)], axis=1)


def setup_inputs():
    n = np.random.standard_normal
    s = mx_kscale(K)[:, None]
    u = mx_kscale(H)
    slot_token = np.empty(E * C, np.int64); pos = np.tile(E * C + np.arange(T) % PAD, (TOP, 1)); taken = np.zeros(T, np.int64)
    liked = np.random.randn(T)
    for e in np.random.permutation(E):
        free = np.flatnonzero(taken < TOP); pick = np.random.permutation(free[np.argsort(-(liked[free] + np.random.gumbel(size=free.size)))[:C]]); slot_token[e * C:(e + 1) * C] = pick
        pos[taken[pick], pick] = e * C + np.arange(C); taken[pick] += 1
    g = np.random.uniform(0.2, 0.8, (TOP, T))
    return {
        "xT": (n((K, T)) * s).astype(np.float32),
        "w1": (n((E, K, H)) / np.sqrt(K) / s[None] * u[None, None, :]).astype(np.float32),
        "w2": (n((E, H, N)) / np.sqrt(H) / u[None, :, None]).astype(np.float32),
        "gate": np.stack([np.tile(r, (N, 1)) for r in g]).astype(np.float32),
        "offs": striped(slot_token),
        "pos1": striped(pos[0]),
        "pos2": striped(pos[1]),
        "pos3": striped(pos[2]),
    }


def reference(xT, w1, w2, gate, offs, pos1, pos2, pos3):
    idx = unstriped(offs)
    xq = mxq(f64(xT)[:, idx], 0, "e4m3")
    h = silu(by_expert(mxq(f64(w1), 1, "e4m3"), xq))
    y = by_expert(mxq(f64(w2), 1, "e4m3"), mxq(h, 0, "e4m3"))
    y = np.concatenate([y, np.zeros((N, PAD))], axis=1)
    return sum(f64(gate[r]) * y[:, unstriped(p)] for r, p in enumerate((pos1, pos2, pos3)))

@@ -1,0 +1,261 @@
+from contextlib import ExitStack
+
+import concourse.mybir as mybir
+from concourse.masks import make_identity
+
+K, T, E, C, H, N = 512, 1280, 8, 256, 512, 256
+TOP = 3
+PAD = 64
+SLOTS = E * C
+
+FLOPS = 2 * SLOTS * (K * H + H * N)
+BYTES = 4 * (K * T + E * K * H + E * H * N + TOP * T + N * T) + 2 * 128 * (SLOTS + TOP * T) // 16
+
+F32 = mybir.dt.float32
+BF16 = mybir.dt.bfloat16
+I32 = mybir.dt.int32
+U32 = mybir.dt.uint32
+U16 = mybir.dt.uint16
+U8 = mybir.dt.uint8
+FP8X4 = mybir.dt.float8_e4m3fn_x4
+COPY = mybir.ActivationFunctionType.Copy
+SILU = mybir.ActivationFunctionType.Silu
+MULT = mybir.AluOpType.mult
+ADD = mybir.AluOpType.add
+
+P = 128
+PACK = 4
+LIST_COL = 16
+BANK = 512
+TOKEN_CHUNKS = ((0, 512), (512, 512), (1024, 256))
+X_PIECES = ((0, 512, True), (512, 512, True), (1024, 256, True))
+GATE_ROWS = 32
+GATE_RUN = T // GATE_ROWS
+GATE_ON_VECTOR = ()
+W2_LAG = 1
+LAST_CHUNKS = ((0, 512), (512, 384), (896, 256), (1152, 128))
+W1_SLOTS = 2
+W1_ON_VECTOR = ((0, 1), (1, 1), (2, 1), (3, 1), (4, 1), (5, 1), (6, 1), (7, 1))
+W2A_ON_VECTOR = (3, 7)
+
+
+def tile_moe_ecr_mlp_silu_kernel(tc, xT, w1, w2, gate, offs, pos1, pos2, pos3, out):
+    nc = tc.nc
+
+    with ExitStack() as ctx:
+        lists = ctx.enter_context(tc.tile_pool(name="lists", bufs=1))
+        keep = ctx.enter_context(tc.tile_pool(name="keep", bufs=1))
+        ring = ctx.enter_context(tc.tile_pool(name="ring", bufs=2))
+        psum = ctx.enter_context(tc.psum_pool(name="psum", bufs=2))
+
+        def cast(on_vector, dst, src):
+            if on_vector:
+                nc.vector.tensor_copy(out=dst, in_=src)
+            else:
+                nc.scalar.activation(out=dst, in_=src, func=COPY)
+
+        def cast_interleave(on_vector, dst, src):
+            cast(
+                on_vector,
+                dst.rearrange("p (c i) j -> p c j i", i=4),
+                src.rearrange("p j (c i) -> p c j i", i=4),
+            )
+
+        def quantize(words, scales, packed):
+            nc.vector.quantize_mx(out=words.bitcast(FP8X4), scales=scales, in_=packed)
+
+        gate_rows = keep.tile([P, P], F32, name="gate_rows")
+        nc.sync.dma_start(
+            out=gate_rows[0:GATE_ROWS, 0 : TOP * GATE_RUN].rearrange("b (r i) -> b r i", r=TOP),
+            in_=gate[:, 0, :].rearrange("r (b i) -> b r i", i=GATE_RUN),
+        )
+        x_raw = []
+        for c0, width in TOKEN_CHUNKS:
+            raw = keep.tile([P, PACK, width], F32, name=f"x_raw{c0}")
+            nc.sync.dma_start(out=raw[:], in_=xT.rearrange("(p j) t -> p j t", j=PACK)[:, :, c0 : c0 + width])
+            x_raw.append(raw)
+        offs_sb = lists.tile([P, SLOTS // LIST_COL], U16, name="offs_sb")
+        nc.sync.dma_start(offs_sb[:], offs)
+
+        def load_w2(half, e):
+            raw = keep.tile([P, PACK, P], F32, name=f"w2_raw{half}_{e}")
+            nc.sync.dma_start(out=raw[:], in_=w2[e].rearrange("(p j) n -> p j n", j=PACK)[:, :, half * P : (half + 1) * P])
+            return raw
+
+        w1_raw = []
+        w2_raw = [[], []]
+        for e in range(E):
+            raw = keep.tile([P, PACK, H], F32, name=f"w1_raw{e}", align_bytes=64)
+            nc.sync.dma_start(out=raw[:], in_=w1[e].rearrange("(p j) i -> p j i", j=PACK))
+            w1_raw.append(raw)
+            if e >= W2_LAG:
+                w2_raw[0].append(load_w2(0, e - W2_LAG))
+        for e in range(E - W2_LAG, E):
+            w2_raw[0].append(load_w2(0, e))
+        pos_sb = []
+        for r, pos in enumerate((pos1, pos2, pos3)):
+            pos_tile = lists.tile([P, T // LIST_COL], U16, name=f"pos_sb{r}")
+            nc.sync.dma_start(pos_tile[:], pos)
+            pos_sb.append(pos_tile)
+        for e in range(E):
+            w2_raw[1].append(load_w2(1, e))
+
+        zeros = keep.tile([P, PAD], F32, name="zeros")
+        nc.vector.memset(zeros[:], 0.0)
+        nc.gpsimd.memset(gate_rows[0:GATE_ROWS, TOP * GATE_RUN :], 0.0)
+        nc.gpsimd.memset(gate_rows[GATE_ROWS : 2 * GATE_ROWS, :], 0.0)
+        nc.gpsimd.memset(gate_rows[2 * GATE_ROWS :, :], 0.0)
+        ident = keep.tile([P, P], F32, name="ident")
+        make_identity(nc, ident[:])
+        y = [keep.tile([P, SLOTS + PAD], F32, name=f"y{half}") for half in range(N // P)]
+        for half in range(N // P):
+            nc.scalar.activation(out=y[half][:, SLOTS:], in_=zeros[:], func=SILU)
+
+        x_words = keep.tile([P, T], U32, name="x_words", align_bytes=64)
+        x_scales = keep.tile([P, T], U8, name="x_scales", align_bytes=64)
+        nc.vector.memset(x_scales[:].bitcast(I32), 0)
+        for t0, width, on_vector in X_PIECES:
+            chunk = t0 // BANK
+            a = t0 - chunk * BANK
+            packed = keep.tile([P, width, PACK], BF16, name=f"x_packed{t0}", align_bytes=64)
+            cast_interleave(on_vector, packed[:], x_raw[chunk][:, :, a : a + width])
+            quantize(x_words[:, t0 : t0 + width], x_scales[:, t0 : t0 + width], packed[:].rearrange("p t j -> p (t j)"))
+
+        h_words = []
+        h_scales = []
+
+        def second_layer(half, first, count, packed):
+            for i in range(count):
+                cast_interleave(half == 0 and first + i in W2A_ON_VECTOR, packed[:, i, :, :], w2_raw[half][first + i][:])
+            words = ring.tile([P, count * P], U32, name="w2_words", align_bytes=64)
+            scales = ring.tile([P, count * P], U8, name="w2_scales", align_bytes=64)
+            quantize(words[:], scales[:], packed.rearrange("p e n j -> p (e n j)"))
+            for i0 in range(0, count, 2):
+                acc = psum.tile([P, 2, C], F32, name="acc", tag="acc")
+                for i in (i0, i0 + 1):
+                    nc.tensor.matmul_mx(
+                        out=acc[:, i - i0, :],
+                        lhsT=words[:, i * P : (i + 1) * P].bitcast(FP8X4),
+                        lhsT_scale=scales[:, i * P : (i + 1) * P],
+                        rhs=h_words[first + i][:].bitcast(FP8X4),
+                        rhs_scale=h_scales[first + i][:],
+                        start=True,
+                        stop=True,
+                    )
+                e0 = first + i0
+                nc.scalar.copy(out=y[half][:, e0 * C : (e0 + 2) * C], in_=acc[:].rearrange("p e s -> p (e s)"))
+
+        w1_packed = [keep.tile([P, PACK, P, PACK], BF16, name=f"w1_packed{i}", align_bytes=64) for i in range(W1_SLOTS)]
+        spent = [raw[:].rearrange("p j i -> p (j i)").bitcast(BF16) for raw in w1_raw]
+
+        def prepare(e):
+            slot_words = ring.tile([P, C], U32, name="slot_words", bufs=2, align_bytes=64)
+            slot_scales = ring.tile([P, C], U8, name="slot_scales", bufs=2, align_bytes=64)
+            entries = offs_sb[:, e * C // LIST_COL : (e + 1) * C // LIST_COL]
+            nc.vector.tensor_copy(out=slot_words[:], in_=x_words[:].indirect(entries))
+            nc.vector.tensor_copy(out=slot_scales[:], in_=x_scales[:].indirect(entries))
+            packed = w1_packed[e % W1_SLOTS]
+            for u in range(2):
+                cast(
+                    (e, u) in W1_ON_VECTOR,
+                    packed[:, 2 * u : 2 * u + 2, :, :].rearrange("p t m j -> p m j t"),
+                    w1_raw[e][:].rearrange("p j (m t) -> p m j t", t=PACK)[:, :, :, 2 * u : 2 * u + 2],
+                )
+            w_words = ring.tile([P, H], U32, name="w1_words", align_bytes=64)
+            w_scales = ring.tile([P, H], U8, name="w1_scales", align_bytes=64)
+            quantize(w_words[:], w_scales[:], packed[:].rearrange("p t m j -> p (t m j)"))
+            return slot_words, slot_scales, w_words, w_scales
+
+        def first_layer(e, slot_words, slot_scales, w_words, w_scales):
+            h_flat = spent[min(e + 1, E - 1)][:, (e % 4) * C * PACK : (e % 4 + 1) * C * PACK]
+            h_packed = h_flat.rearrange("p (s t) -> p s t", t=PACK)
+            for s0 in range(0, C, P):
+                a = psum.tile([P, PACK, P], F32, name="a", tag="four", bufs=4)
+                for t in range(PACK):
+                    cols = slice(t * P, (t + 1) * P)
+                    nc.tensor.matmul_mx(
+                        out=a[:, t, :],
+                        lhsT=w_words[:, cols].bitcast(FP8X4),
+                        lhsT_scale=w_scales[:, cols],
+                        rhs=slot_words[:, s0 : s0 + P].bitcast(FP8X4),
+                        rhs_scale=slot_scales[:, s0 : s0 + P],
+                        start=True,
+                        stop=True,
+                    )
+                nc.scalar.activation(out=h_packed[:, s0 : s0 + P, :], in_=a[:].rearrange("p t s -> p s t"), func=SILU)
+            words = keep.tile([P, C], U32, name=f"h_words{e}", align_bytes=64)
+            scales = keep.tile([P, C], U8, name=f"h_scales{e}", align_bytes=64)
+            quantize(words[:], scales[:], h_flat)
+            h_words.append(words)
+            h_scales.append(scales)
+
+        ready = prepare(0)
+        for e in range(E):
+            operands = ready
+            if e + 1 < E:
+                ready = prepare(e + 1)
+            first_layer(e, *operands)
+            if e % 2 == 1:
+                w2_packed = ring.tile([P, 2, P, PACK], BF16, name="w2_packed", align_bytes=64)
+                second_layer(0, e - 1, 2, w2_packed[:])
+
+        turned = psum.tile([P, P], F32, name="turned", tag="two")
+        nc.tensor.transpose(turned[:], gate_rows[:], ident[:])
+        gate_cols = keep.tile([P, GATE_ROWS], F32, name="gate_cols")
+        nc.scalar.copy(out=gate_cols[:], in_=turned[:, 0:GATE_ROWS])
+        gates = keep.tile([P, TOP, T], F32, name="gates")
+        for b0 in range(0, GATE_ROWS, 4):
+            bank = psum.tile([P, 4, P], F32, name="bank", tag="two")
+            for b in range(4):
+                nc.tensor.transpose(bank[:, b, :], gate_cols[:, b0 + b : b0 + b + 1].to_broadcast([P, P]), ident[:])
+            dst = gates[:, :, b0 * GATE_RUN : (b0 + 4) * GATE_RUN].rearrange("p r (b i) -> p b r i", b=4)
+            src = bank[:, :, 0 : TOP * GATE_RUN].rearrange("p b (r i) -> p b r i", r=TOP)
+            if b0 // 4 in GATE_ON_VECTOR:
+                nc.vector.tensor_copy(out=dst, in_=src)
+            else:
+                nc.scalar.copy(out=dst, in_=src)
+
+        def combine(half, c0, width, last, first_product=None):
+            products = []
+            for r in range(TOP):
+                if r == 0 and first_product is not None:
+                    product = first_product
+                else:
+                    product = ring.tile([P, width], F32, name=f"product{r}")[:]
+                entries = pos_sb[r][:, c0 // LIST_COL : (c0 + width) // LIST_COL]
+                nc.vector.tensor_tensor(product, y[half][:].indirect(entries), gates[:, r, c0 : c0 + width], MULT)
+                products.append(product)
+            result = ring.tile([P, width], F32, name="result", bufs=3)
+            if last:
+                partial = ring.tile([P, width], F32, name="summed")
+                nc.vector.tensor_tensor(partial[:], products[0], products[1], ADD)
+                nc.vector.tensor_tensor(result[:], partial[:], products[2], ADD)
+            else:
+                total = psum.tile([P, BANK], F32, name="total", tag="four", bufs=4)
+                for b0 in range(0, width, P):
+                    for r in range(TOP):
+                        nc.tensor.matmul(
+                            total[:, b0 : b0 + P],
+                            lhsT=products[r][:, b0 : b0 + P],
+                            rhs=ident[:],
+                            start=(r == 0),
+                            stop=(r == TOP - 1),
+                            is_transpose=True,
+                        )
+                summed = ring.tile([P, width], F32, name="summed")
+                nc.scalar.copy(out=summed[:], in_=total[:, 0:width])
+                back = psum.tile([P, BANK], F32, name="back", tag="two")
+                for b0 in range(0, width, P):
+                    nc.tensor.transpose(back[:, b0 : b0 + P], summed[:, b0 : b0 + P], ident[:])
+                nc.scalar.copy(out=result[:], in_=back[:, 0:width])
+            nc.sync.dma_start(out=out[half * P : (half + 1) * P, c0 : c0 + width], in_=result[:])
+
+        early = w1_packed[(E - 1) % W1_SLOTS][:]
+        late = spent[E - 1][:, 2 * C * PACK : 4 * C * PACK].rearrange("p (e n j) -> p e n j", n=P, j=PACK)
+        combine(0, 0, 256, False)
+        second_layer(1, 0, E // 2, early)
+        combine(0, 256, 512, False, early.rearrange("p e n j -> p (e n j)").bitcast(F32)[:, 0:512])
+        second_layer(1, E // 2, E // 2, late)
+        combine(0, 768, 512, False, late.rearrange("p e n j -> p (e n j)").bitcast(F32)[:, 0:512])
+        for c0, width in LAST_CHUNKS:
+            combine(1, c0, width, c0 + width == T)

@@ -28,15 +28,24 @@ PACK = 4
 LIST_COL = 16
 BANK = 512
 TOKEN_CHUNKS = ((0, 512), (512, 512), (1024, 256))
-X_PIECES = ((0, 512, True), (512, 512, True), (1024, 256, True))
+X_CHUNKS = ((0, 512), (512, 512), (1024, 256))
+X_PIECES = ((0, 0, 512, True), (1, 0, 256, False), (1, 256, 256, True), (2, 0, 256, True))
 GATE_ROWS = 32
 GATE_RUN = T // GATE_ROWS
-GATE_ON_VECTOR = ()
-W2_LAG = 1
-LAST_CHUNKS = ((0, 512), (512, 384), (896, 256), (1152, 128))
+GATE_EARLY = 12
+W2_LAG = 3
+LAST_CHUNKS = ((0, 384), (384, 384), (768, 256), (1024, 256))
+AHEAD = 2
+SECOND_LAG = 0
+Y_ON_VECTOR = (4, 6, 7)
+FIRST_CHUNKS = TOKEN_CHUNKS
 W1_SLOTS = 2
-W1_ON_VECTOR = ((0, 1), (1, 1), (2, 1), (3, 1), (4, 1), (5, 1), (6, 1), (7, 1))
-W2A_ON_VECTOR = (3, 7)
+GATHERS = {0: 1, 1: 1, 2: 1, 3: 1, 4: 1, 5: 1, 6: 1, 7: 1}
+ON_SCALAR = ((0, 4, False),)
+ON_VECTOR = ((0, 4, True),)
+SHARED = ((0, 2, False), (2, 4, True))
+W1_CUTS = (ON_SCALAR,) + (SHARED,) * 6 + (ON_VECTOR,)
+W2_ON_VECTOR = ((0, 2), (0, 3), (0, 4), (0, 5), (0, 6), (0, 7))
 
 
 def tile_moe_ecr_mlp_silu_kernel(tc, xT, w1, w2, gate, offs, pos1, pos2, pos3, out):
@@ -70,35 +79,33 @@ def tile_moe_ecr_mlp_silu_kernel(tc, xT, w1, w2, gate, offs, pos1, pos2, pos3, o
             in_=gate[:, 0, :].rearrange("r (b i) -> b r i", i=GATE_RUN),
         )
         x_raw = []
-        for c0, width in TOKEN_CHUNKS:
+        for c0, width in X_CHUNKS:
             raw = keep.tile([P, PACK, width], F32, name=f"x_raw{c0}")
             nc.sync.dma_start(out=raw[:], in_=xT.rearrange("(p j) t -> p j t", j=PACK)[:, :, c0 : c0 + width])
             x_raw.append(raw)
         offs_sb = lists.tile([P, SLOTS // LIST_COL], U16, name="offs_sb")
         nc.sync.dma_start(offs_sb[:], offs)
 
-        def load_w2(half, e):
-            raw = keep.tile([P, PACK, P], F32, name=f"w2_raw{half}_{e}")
-            nc.sync.dma_start(out=raw[:], in_=w2[e].rearrange("(p j) n -> p j n", j=PACK)[:, :, half * P : (half + 1) * P])
+        def load_w2(e):
+            raw = keep.tile([P, PACK, N], F32, name=f"w2_raw{e}")
+            nc.sync.dma_start(out=raw[:], in_=w2[e].rearrange("(p j) n -> p j n", j=PACK))
             return raw
 
         w1_raw = []
-        w2_raw = [[], []]
+        w2_raw = []
         for e in range(E):
             raw = keep.tile([P, PACK, H], F32, name=f"w1_raw{e}", align_bytes=64)
             nc.sync.dma_start(out=raw[:], in_=w1[e].rearrange("(p j) i -> p j i", j=PACK))
             w1_raw.append(raw)
             if e >= W2_LAG:
-                w2_raw[0].append(load_w2(0, e - W2_LAG))
+                w2_raw.append(load_w2(e - W2_LAG))
         for e in range(E - W2_LAG, E):
-            w2_raw[0].append(load_w2(0, e))
+            w2_raw.append(load_w2(e))
         pos_sb = []
         for r, pos in enumerate((pos1, pos2, pos3)):
             pos_tile = lists.tile([P, T // LIST_COL], U16, name=f"pos_sb{r}")
             nc.sync.dma_start(pos_tile[:], pos)
             pos_sb.append(pos_tile)
-        for e in range(E):
-            w2_raw[1].append(load_w2(1, e))
 
         zeros = keep.tile([P, PAD], F32, name="zeros")
         nc.vector.memset(zeros[:], 0.0)
@@ -114,25 +121,45 @@ def tile_moe_ecr_mlp_silu_kernel(tc, xT, w1, w2, gate, offs, pos1, pos2, pos3, o
         x_words = keep.tile([P, T], U32, name="x_words", align_bytes=64)
         x_scales = keep.tile([P, T], U8, name="x_scales", align_bytes=64)
         nc.vector.memset(x_scales[:].bitcast(I32), 0)
-        for t0, width, on_vector in X_PIECES:
-            chunk = t0 // BANK
-            a = t0 - chunk * BANK
+        for chunk, a, width, on_vector in X_PIECES:
+            t0 = X_CHUNKS[chunk][0] + a
             packed = keep.tile([P, width, PACK], BF16, name=f"x_packed{t0}", align_bytes=64)
             cast_interleave(on_vector, packed[:], x_raw[chunk][:, :, a : a + width])
             quantize(x_words[:, t0 : t0 + width], x_scales[:, t0 : t0 + width], packed[:].rearrange("p t j -> p (t j)"))
 
+        turned = psum.tile([P, P], F32, name="turned", tag="two")
+        nc.tensor.transpose(turned[:], gate_rows[:], ident[:])
+        gate_cols = keep.tile([P, GATE_ROWS], F32, name="gate_cols")
+        nc.scalar.copy(out=gate_cols[:], in_=turned[:, 0:GATE_ROWS])
+        gates = keep.tile([P, TOP, T], F32, name="gates")
+
+        def spread_gates(b0):
+            bank = psum.tile([P, 4, P], F32, name="bank", tag="two")
+            for b in range(4):
+                nc.tensor.transpose(bank[:, b, :], gate_cols[:, b0 + b : b0 + b + 1].to_broadcast([P, P]), ident[:])
+            dst = gates[:, :, b0 * GATE_RUN : (b0 + 4) * GATE_RUN].rearrange("p r (b i) -> p b r i", b=4)
+            src = bank[:, :, 0 : TOP * GATE_RUN].rearrange("p b (r i) -> p b r i", r=TOP)
+            nc.scalar.copy(out=dst, in_=src)
+
+        for b0 in range(0, GATE_EARLY, 4):
+            spread_gates(b0)
+
         h_words = []
         h_scales = []
 
-        def second_layer(half, first, count, packed):
+        def second_weights(half, first, count, packed):
             for i in range(count):
-                cast_interleave(half == 0 and first + i in W2A_ON_VECTOR, packed[:, i, :, :], w2_raw[half][first + i][:])
+                cast_interleave((half, first + i) in W2_ON_VECTOR, packed[:, i, :, :], w2_raw[first + i][:, :, half * P : (half + 1) * P])
             words = ring.tile([P, count * P], U32, name="w2_words", align_bytes=64)
             scales = ring.tile([P, count * P], U8, name="w2_scales", align_bytes=64)
             quantize(words[:], scales[:], packed.rearrange("p e n j -> p (e n j)"))
-            for i0 in range(0, count, 2):
-                acc = psum.tile([P, 2, C], F32, name="acc", tag="acc")
-                for i in (i0, i0 + 1):
+            return words, scales
+
+        def second_layer(half, first, count, words, scales):
+            step = 1 if (half, first + count) == (0, E) else 2
+            for i0 in range(0, count, step):
+                acc = psum.tile([P, step, C], F32, name="acc", tag="acc")
+                for i in range(i0, i0 + step):
                     nc.tensor.matmul_mx(
                         out=acc[:, i - i0, :],
                         lhsT=words[:, i * P : (i + 1) * P].bitcast(FP8X4),
@@ -143,31 +170,42 @@ def tile_moe_ecr_mlp_silu_kernel(tc, xT, w1, w2, gate, offs, pos1, pos2, pos3, o
                         stop=True,
                     )
                 e0 = first + i0
-                nc.scalar.copy(out=y[half][:, e0 * C : (e0 + 2) * C], in_=acc[:].rearrange("p e s -> p (e s)"))
+                dst = y[half][:, e0 * C : (e0 + step) * C]
+                if half == 0 and e0 in Y_ON_VECTOR:
+                    nc.vector.tensor_copy(out=dst, in_=acc[:].rearrange("p e s -> p (e s)"))
+                else:
+                    nc.scalar.copy(out=dst, in_=acc[:].rearrange("p e s -> p (e s)"))
 
         w1_packed = [keep.tile([P, PACK, P, PACK], BF16, name=f"w1_packed{i}", align_bytes=64) for i in range(W1_SLOTS)]
         spent = [raw[:].rearrange("p j i -> p (j i)").bitcast(BF16) for raw in w1_raw]
 
+        gathered = []
+
         def prepare(e):
-            slot_words = ring.tile([P, C], U32, name="slot_words", bufs=2, align_bytes=64)
-            slot_scales = ring.tile([P, C], U8, name="slot_scales", bufs=2, align_bytes=64)
-            entries = offs_sb[:, e * C // LIST_COL : (e + 1) * C // LIST_COL]
-            nc.vector.tensor_copy(out=slot_words[:], in_=x_words[:].indirect(entries))
-            nc.vector.tensor_copy(out=slot_scales[:], in_=x_scales[:].indirect(entries))
+            if e in GATHERS:
+                count = GATHERS[e] * C
+                slot_words = ring.tile([P, count], U32, name="slot_words", bufs=3, align_bytes=64)
+                slot_scales = ring.tile([P, count], U8, name="slot_scales", bufs=3, align_bytes=64)
+                entries = offs_sb[:, e * C // LIST_COL : (e * C + count) // LIST_COL]
+                nc.vector.tensor_copy(out=slot_words[:], in_=x_words[:].indirect(entries))
+                nc.vector.tensor_copy(out=slot_scales[:], in_=x_scales[:].indirect(entries))
+                for i in range(GATHERS[e]):
+                    gathered.append((slot_words[:, i * C : (i + 1) * C], slot_scales[:, i * C : (i + 1) * C]))
+            slot_words, slot_scales = gathered[e]
             packed = w1_packed[e % W1_SLOTS]
-            for u in range(2):
+            for t0, t1, on_vector in W1_CUTS[e]:
                 cast(
-                    (e, u) in W1_ON_VECTOR,
-                    packed[:, 2 * u : 2 * u + 2, :, :].rearrange("p t m j -> p m j t"),
-                    w1_raw[e][:].rearrange("p j (m t) -> p m j t", t=PACK)[:, :, :, 2 * u : 2 * u + 2],
+                    on_vector,
+                    packed[:, t0:t1, :, :].rearrange("p t m j -> p m j t"),
+                    w1_raw[e][:].rearrange("p j (m t) -> p m j t", t=PACK)[:, :, :, t0:t1],
                 )
-            w_words = ring.tile([P, H], U32, name="w1_words", align_bytes=64)
-            w_scales = ring.tile([P, H], U8, name="w1_scales", align_bytes=64)
+            w_words = ring.tile([P, H], U32, name="w1_words", bufs=3, align_bytes=64)
+            w_scales = ring.tile([P, H], U8, name="w1_scales", bufs=3, align_bytes=64)
             quantize(w_words[:], w_scales[:], packed[:].rearrange("p t m j -> p (t m j)"))
             return slot_words, slot_scales, w_words, w_scales
 
         def first_layer(e, slot_words, slot_scales, w_words, w_scales):
-            h_flat = spent[min(e + 1, E - 1)][:, (e % 4) * C * PACK : (e % 4 + 1) * C * PACK]
+            h_flat = spent[min(e + 0, E - 1)][:, (e % 4) * C * PACK : (e % 4 + 1) * C * PACK]
             h_packed = h_flat.rearrange("p (s t) -> p s t", t=PACK)
             for s0 in range(0, C, P):
                 a = psum.tile([P, PACK, P], F32, name="a", tag="four", bufs=4)
@@ -189,43 +227,28 @@ def tile_moe_ecr_mlp_silu_kernel(tc, xT, w1, w2, gate, offs, pos1, pos2, pos3, o
             h_words.append(words)
             h_scales.append(scales)
 
-        ready = prepare(0)
-        for e in range(E):
-            operands = ready
-            if e + 1 < E:
-                ready = prepare(e + 1)
-            first_layer(e, *operands)
-            if e % 2 == 1:
+        ready = [prepare(e) for e in range(AHEAD)]
+        for e in range(E + SECOND_LAG):
+            if e + AHEAD < E:
+                ready.append(prepare(e + AHEAD))
+            if e < E:
+                first_layer(e, *ready[e])
+            if e >= SECOND_LAG and (e - SECOND_LAG) % 2 == 1:
                 w2_packed = ring.tile([P, 2, P, PACK], BF16, name="w2_packed", align_bytes=64)
-                second_layer(0, e - 1, 2, w2_packed[:])
+                first = e - SECOND_LAG - 1
+                second_layer(0, first, 2, *second_weights(0, first, 2, w2_packed[:]))
 
-        turned = psum.tile([P, P], F32, name="turned", tag="two")
-        nc.tensor.transpose(turned[:], gate_rows[:], ident[:])
-        gate_cols = keep.tile([P, GATE_ROWS], F32, name="gate_cols")
-        nc.scalar.copy(out=gate_cols[:], in_=turned[:, 0:GATE_ROWS])
-        gates = keep.tile([P, TOP, T], F32, name="gates")
-        for b0 in range(0, GATE_ROWS, 4):
-            bank = psum.tile([P, 4, P], F32, name="bank", tag="two")
-            for b in range(4):
-                nc.tensor.transpose(bank[:, b, :], gate_cols[:, b0 + b : b0 + b + 1].to_broadcast([P, P]), ident[:])
-            dst = gates[:, :, b0 * GATE_RUN : (b0 + 4) * GATE_RUN].rearrange("p r (b i) -> p b r i", b=4)
-            src = bank[:, :, 0 : TOP * GATE_RUN].rearrange("p b (r i) -> p b r i", r=TOP)
-            if b0 // 4 in GATE_ON_VECTOR:
-                nc.vector.tensor_copy(out=dst, in_=src)
-            else:
-                nc.scalar.copy(out=dst, in_=src)
-
-        def combine(half, c0, width, last, first_product=None):
+        def combine(half, c0, width, last, given=()):
             products = []
             for r in range(TOP):
-                if r == 0 and first_product is not None:
-                    product = first_product
+                if r < len(given):
+                    product = given[r]
                 else:
                     product = ring.tile([P, width], F32, name=f"product{r}")[:]
                 entries = pos_sb[r][:, c0 // LIST_COL : (c0 + width) // LIST_COL]
                 nc.vector.tensor_tensor(product, y[half][:].indirect(entries), gates[:, r, c0 : c0 + width], MULT)
                 products.append(product)
-            result = ring.tile([P, width], F32, name="result", bufs=3)
+            result = ring.tile([P, width], F32, name="result", bufs=4)
             if last:
                 partial = ring.tile([P, width], F32, name="summed")
                 nc.vector.tensor_tensor(partial[:], products[0], products[1], ADD)
@@ -250,12 +273,13 @@ def tile_moe_ecr_mlp_silu_kernel(tc, xT, w1, w2, gate, offs, pos1, pos2, pos3, o
                 nc.scalar.copy(out=result[:], in_=back[:, 0:width])
             nc.sync.dma_start(out=out[half * P : (half + 1) * P, c0 : c0 + width], in_=result[:])
 
-        early = w1_packed[(E - 1) % W1_SLOTS][:]
-        late = spent[E - 1][:, 2 * C * PACK : 4 * C * PACK].rearrange("p (e n j) -> p e n j", n=P, j=PACK)
-        combine(0, 0, 256, False)
-        second_layer(1, 0, E // 2, early)
-        combine(0, 256, 512, False, early.rearrange("p e n j -> p (e n j)").bitcast(F32)[:, 0:512])
-        second_layer(1, E // 2, E // 2, late)
-        combine(0, 768, 512, False, late.rearrange("p e n j -> p (e n j)").bitcast(F32)[:, 0:512])
+        for b0 in range(GATE_EARLY, GATE_ROWS, 4):
+            spread_gates(b0)
+        late = spent[E - 1]
+        upper = second_weights(1, 0, E, late.rearrange("p (e n j) -> p e n j", n=P, j=PACK))
+        combine(0, 0, 384, False)
+        second_layer(1, 0, E, *upper)
+        combine(0, 384, 512, False, [late.bitcast(F32)[:, r * 512 : (r + 1) * 512] for r in range(TOP)])
+        combine(0, 384 + 512, 768 - 384, False)
         for c0, width in LAST_CHUNKS:
-            combine(1, c0, width, c0 + width == T)
+            combine(1, c0, width, c0 >= 1024)

@@ -33,19 +33,20 @@ X_PIECES = ((0, 0, 512, True), (1, 0, 256, False), (1, 256, 256, True), (2, 0, 2
 GATE_ROWS = 32
 GATE_RUN = T // GATE_ROWS
 GATE_EARLY = 12
-W2_LAG = 3
+W2_LAG = 4
 LAST_CHUNKS = ((0, 384), (384, 384), (768, 256), (1024, 256))
-AHEAD = 2
-SECOND_LAG = 0
-Y_ON_VECTOR = (4, 6, 7)
+AHEAD = 1
+SECOND_LAG = 1
+Y_ON_VECTOR = (6, 7)
 FIRST_CHUNKS = TOKEN_CHUNKS
-W1_SLOTS = 2
+W1_SLOTS = 3
 GATHERS = {0: 1, 1: 1, 2: 1, 3: 1, 4: 1, 5: 1, 6: 1, 7: 1}
+SCALE_GATHERS = {0: 2, 2: 2, 4: 2, 6: 2}
 ON_SCALAR = ((0, 4, False),)
 ON_VECTOR = ((0, 4, True),)
 SHARED = ((0, 2, False), (2, 4, True))
 W1_CUTS = (ON_SCALAR,) + (SHARED,) * 6 + (ON_VECTOR,)
-W2_ON_VECTOR = ((0, 2), (0, 3), (0, 4), (0, 5), (0, 6), (0, 7))
+W2_ON_VECTOR = ((0, 4), (0, 5), (0, 6), (0, 7))
 
 
 def tile_moe_ecr_mlp_silu_kernel(tc, xT, w1, w2, gate, offs, pos1, pos2, pos3, out):
@@ -155,10 +156,15 @@ def tile_moe_ecr_mlp_silu_kernel(tc, xT, w1, w2, gate, offs, pos1, pos2, pos3, o
             quantize(words[:], scales[:], packed.rearrange("p e n j -> p (e n j)"))
             return words, scales
 
+        def acc_tag(half, e0):
+            if half == 0:
+                return f"acc{e0 // (2 - (e0 >= E - 2)) % 2}"
+            return ("acc0", "acc1", "bank2", "bank3")[e0 // 2]
+
         def second_layer(half, first, count, words, scales):
             step = 1 if (half, first + count) == (0, E) else 2
             for i0 in range(0, count, step):
-                acc = psum.tile([P, step, C], F32, name="acc", tag="acc")
+                acc = psum.tile([P, step, C], F32, name="acc", tag=acc_tag(half, first + i0), bufs=1)
                 for i in range(i0, i0 + step):
                     nc.tensor.matmul_mx(
                         out=acc[:, i - i0, :],
@@ -176,7 +182,6 @@ def tile_moe_ecr_mlp_silu_kernel(tc, xT, w1, w2, gate, offs, pos1, pos2, pos3, o
                 else:
                     nc.scalar.copy(out=dst, in_=acc[:].rearrange("p e s -> p (e s)"))
 
-        w1_packed = [keep.tile([P, PACK, P, PACK], BF16, name=f"w1_packed{i}", align_bytes=64) for i in range(W1_SLOTS)]
         spent = [raw[:].rearrange("p j i -> p (j i)").bitcast(BF16) for raw in w1_raw]
 
         gathered = []
@@ -184,31 +189,35 @@ def tile_moe_ecr_mlp_silu_kernel(tc, xT, w1, w2, gate, offs, pos1, pos2, pos3, o
         def prepare(e):
             if e in GATHERS:
                 count = GATHERS[e] * C
-                slot_words = ring.tile([P, count], U32, name="slot_words", bufs=3, align_bytes=64)
-                slot_scales = ring.tile([P, count], U8, name="slot_scales", bufs=3, align_bytes=64)
+                tag = f"stage{(e - 1) % W1_SLOTS}" if e >= 2 else f"first{e}"
+                slot_words = keep.tile([P, count], U32, name="slot_words", tag=tag, align_bytes=64)
                 entries = offs_sb[:, e * C // LIST_COL : (e * C + count) // LIST_COL]
                 nc.vector.tensor_copy(out=slot_words[:], in_=x_words[:].indirect(entries))
-                nc.vector.tensor_copy(out=slot_scales[:], in_=x_scales[:].indirect(entries))
-                for i in range(GATHERS[e]):
-                    gathered.append((slot_words[:, i * C : (i + 1) * C], slot_scales[:, i * C : (i + 1) * C]))
-            slot_words, slot_scales = gathered[e]
-            packed = w1_packed[e % W1_SLOTS]
+            if e in SCALE_GATHERS:
+                count = SCALE_GATHERS[e] * C
+                some_scales = ring.tile([P, count], U8, name="slot_scales", bufs=2, align_bytes=64)
+                entries = offs_sb[:, e * C // LIST_COL : (e * C + count) // LIST_COL]
+                nc.vector.tensor_copy(out=some_scales[:], in_=x_scales[:].indirect(entries))
+                for i in range(SCALE_GATHERS[e]):
+                    gathered.append(some_scales[:, i * C : (i + 1) * C])
+            slot_scales = gathered[e]
+            packed = keep.tile([P, PACK, P, PACK], BF16, name="w1_packed", tag=f"stage{e % W1_SLOTS}", align_bytes=64)
             for t0, t1, on_vector in W1_CUTS[e]:
                 cast(
                     on_vector,
                     packed[:, t0:t1, :, :].rearrange("p t m j -> p m j t"),
                     w1_raw[e][:].rearrange("p j (m t) -> p m j t", t=PACK)[:, :, :, t0:t1],
                 )
-            w_words = ring.tile([P, H], U32, name="w1_words", bufs=3, align_bytes=64)
-            w_scales = ring.tile([P, H], U8, name="w1_scales", bufs=3, align_bytes=64)
+            w_words = ring.tile([P, H], U32, name="w1_words", bufs=2, align_bytes=64)
+            w_scales = ring.tile([P, H], U8, name="w1_scales", bufs=2, align_bytes=64)
             quantize(w_words[:], w_scales[:], packed[:].rearrange("p t m j -> p (t m j)"))
             return slot_words, slot_scales, w_words, w_scales
 
         def first_layer(e, slot_words, slot_scales, w_words, w_scales):
-            h_flat = spent[min(e + 0, E - 1)][:, (e % 4) * C * PACK : (e % 4 + 1) * C * PACK]
+            h_flat = spent[min(e + 1, E - 1)][:, (e % 4) * C * PACK : (e % 4 + 1) * C * PACK]
             h_packed = h_flat.rearrange("p (s t) -> p s t", t=PACK)
             for s0 in range(0, C, P):
-                a = psum.tile([P, PACK, P], F32, name="a", tag="four", bufs=4)
+                a = psum.tile([P, PACK, P], F32, name="a", tag=f"bank{(2 * e + s0 // P) % 4}", bufs=1)
                 for t in range(PACK):
                     cols = slice(t * P, (t + 1) * P)
                     nc.tensor.matmul_mx(
@@ -238,6 +247,8 @@ def tile_moe_ecr_mlp_silu_kernel(tc, xT, w1, w2, gate, offs, pos1, pos2, pos3, o
                 first = e - SECOND_LAG - 1
                 second_layer(0, first, 2, *second_weights(0, first, 2, w2_packed[:]))
 
+        totals = []
+
         def combine(half, c0, width, last, given=()):
             products = []
             for r in range(TOP):
@@ -254,7 +265,8 @@ def tile_moe_ecr_mlp_silu_kernel(tc, xT, w1, w2, gate, offs, pos1, pos2, pos3, o
                 nc.vector.tensor_tensor(partial[:], products[0], products[1], ADD)
                 nc.vector.tensor_tensor(result[:], partial[:], products[2], ADD)
             else:
-                total = psum.tile([P, BANK], F32, name="total", tag="four", bufs=4)
+                total = psum.tile([P, BANK], F32, name="total", tag=f"bank{len(totals) % 2}", bufs=1)
+                totals.append(total)
                 for b0 in range(0, width, P):
                     for r in range(TOP):
                         nc.tensor.matmul(
@@ -280,6 +292,6 @@ def tile_moe_ecr_mlp_silu_kernel(tc, xT, w1, w2, gate, offs, pos1, pos2, pos3, o
         combine(0, 0, 384, False)
         second_layer(1, 0, E, *upper)
         combine(0, 384, 512, False, [late.bitcast(F32)[:, r * 512 : (r + 1) * 512] for r in range(TOP)])
-        combine(0, 384 + 512, 768 - 384, False)
+        combine(0, 384 + 512, 768 - 384, False, [late.bitcast(F32)[:, 1536 : 1536 + 768 - 384]])
         for c0, width in LAST_CHUNKS:
             combine(1, c0, width, c0 >= 1024)

from contextlib import ExitStack

import concourse.mybir as mybir
from concourse.masks import make_identity

K, T, E, C, H, N = 512, 1280, 8, 256, 512, 256
TOP = 3
PAD = 64
SLOTS = E * C

FLOPS = 2 * SLOTS * (K * H + H * N)
BYTES = 4 * (K * T + E * K * H + E * H * N + TOP * T + N * T) + 2 * 128 * (SLOTS + TOP * T) // 16

F32 = mybir.dt.float32
BF16 = mybir.dt.bfloat16
I32 = mybir.dt.int32
U32 = mybir.dt.uint32
U16 = mybir.dt.uint16
U8 = mybir.dt.uint8
FP8X4 = mybir.dt.float8_e4m3fn_x4
COPY = mybir.ActivationFunctionType.Copy
SILU = mybir.ActivationFunctionType.Silu
MULT = mybir.AluOpType.mult
ADD = mybir.AluOpType.add

P = 128
PACK = 4
LIST_COL = 16
BANK = 512
TOKEN_CHUNKS = ((0, 512), (512, 512), (1024, 256))
X_CHUNKS = ((0, 512), (512, 512), (1024, 256))
X_PIECES = ((0, 0, 512, True), (1, 0, 256, False), (1, 256, 256, True), (2, 0, 256, True))
GATE_ROWS = 32
GATE_RUN = T // GATE_ROWS
GATE_EARLY = 12
W2_LAG = 4
LAST_CHUNKS = ((0, 384), (384, 384), (768, 256), (1024, 256))
AHEAD = 1
SECOND_LAG = 1
Y_ON_VECTOR = (6, 7)
FIRST_CHUNKS = TOKEN_CHUNKS
W1_SLOTS = 3
GATHERS = {0: 1, 1: 1, 2: 1, 3: 1, 4: 1, 5: 1, 6: 1, 7: 1}
SCALE_GATHERS = {0: 2, 2: 2, 4: 2, 6: 2}
ON_SCALAR = ((0, 4, False),)
ON_VECTOR = ((0, 4, True),)
SHARED = ((0, 2, False), (2, 4, True))
W1_CUTS = (ON_SCALAR,) + (SHARED,) * 6 + (ON_VECTOR,)
W2_ON_VECTOR = ((0, 4), (0, 5), (0, 6), (0, 7))


def tile_moe_ecr_mlp_silu_kernel(tc, xT, w1, w2, gate, offs, pos1, pos2, pos3, out):
    nc = tc.nc

    with ExitStack() as ctx:
        lists = ctx.enter_context(tc.tile_pool(name="lists", bufs=1))
        keep = ctx.enter_context(tc.tile_pool(name="keep", bufs=1))
        ring = ctx.enter_context(tc.tile_pool(name="ring", bufs=2))
        psum = ctx.enter_context(tc.psum_pool(name="psum", bufs=2))

        def cast(on_vector, dst, src):
            if on_vector:
                nc.vector.tensor_copy(out=dst, in_=src)
            else:
                nc.scalar.activation(out=dst, in_=src, func=COPY)

        def cast_interleave(on_vector, dst, src):
            cast(
                on_vector,
                dst.rearrange("p (c i) j -> p c j i", i=4),
                src.rearrange("p j (c i) -> p c j i", i=4),
            )

        def quantize(words, scales, packed):
            nc.vector.quantize_mx(out=words.bitcast(FP8X4), scales=scales, in_=packed)

        gate_rows = keep.tile([P, P], F32, name="gate_rows")
        nc.sync.dma_start(
            out=gate_rows[0:GATE_ROWS, 0 : TOP * GATE_RUN].rearrange("b (r i) -> b r i", r=TOP),
            in_=gate[:, 0, :].rearrange("r (b i) -> b r i", i=GATE_RUN),
        )
        x_raw = []
        for c0, width in X_CHUNKS:
            raw = keep.tile([P, PACK, width], F32, name=f"x_raw{c0}")
            nc.sync.dma_start(out=raw[:], in_=xT.rearrange("(p j) t -> p j t", j=PACK)[:, :, c0 : c0 + width])
            x_raw.append(raw)
        offs_sb = lists.tile([P, SLOTS // LIST_COL], U16, name="offs_sb")
        nc.sync.dma_start(offs_sb[:], offs)

        def load_w2(e):
            raw = keep.tile([P, PACK, N], F32, name=f"w2_raw{e}")
            nc.sync.dma_start(out=raw[:], in_=w2[e].rearrange("(p j) n -> p j n", j=PACK))
            return raw

        w1_raw = []
        w2_raw = []
        for e in range(E):
            raw = keep.tile([P, PACK, H], F32, name=f"w1_raw{e}", align_bytes=64)
            nc.sync.dma_start(out=raw[:], in_=w1[e].rearrange("(p j) i -> p j i", j=PACK))
            w1_raw.append(raw)
            if e >= W2_LAG:
                w2_raw.append(load_w2(e - W2_LAG))
        for e in range(E - W2_LAG, E):
            w2_raw.append(load_w2(e))
        pos_sb = []
        for r, pos in enumerate((pos1, pos2, pos3)):
            pos_tile = lists.tile([P, T // LIST_COL], U16, name=f"pos_sb{r}")
            nc.sync.dma_start(pos_tile[:], pos)
            pos_sb.append(pos_tile)

        zeros = keep.tile([P, PAD], F32, name="zeros")
        nc.vector.memset(zeros[:], 0.0)
        nc.gpsimd.memset(gate_rows[0:GATE_ROWS, TOP * GATE_RUN :], 0.0)
        nc.gpsimd.memset(gate_rows[GATE_ROWS : 2 * GATE_ROWS, :], 0.0)
        nc.gpsimd.memset(gate_rows[2 * GATE_ROWS :, :], 0.0)
        ident = keep.tile([P, P], F32, name="ident")
        make_identity(nc, ident[:])
        y = [keep.tile([P, SLOTS + PAD], F32, name=f"y{half}") for half in range(N // P)]
        for half in range(N // P):
            nc.scalar.activation(out=y[half][:, SLOTS:], in_=zeros[:], func=SILU)

        x_words = keep.tile([P, T], U32, name="x_words", align_bytes=64)
        x_scales = keep.tile([P, T], U8, name="x_scales", align_bytes=64)
        nc.vector.memset(x_scales[:].bitcast(I32), 0)
        for chunk, a, width, on_vector in X_PIECES:
            t0 = X_CHUNKS[chunk][0] + a
            packed = keep.tile([P, width, PACK], BF16, name=f"x_packed{t0}", align_bytes=64)
            cast_interleave(on_vector, packed[:], x_raw[chunk][:, :, a : a + width])
            quantize(x_words[:, t0 : t0 + width], x_scales[:, t0 : t0 + width], packed[:].rearrange("p t j -> p (t j)"))

        turned = psum.tile([P, P], F32, name="turned", tag="two")
        nc.tensor.transpose(turned[:], gate_rows[:], ident[:])
        gate_cols = keep.tile([P, GATE_ROWS], F32, name="gate_cols")
        nc.scalar.copy(out=gate_cols[:], in_=turned[:, 0:GATE_ROWS])
        gates = keep.tile([P, TOP, T], F32, name="gates")

        def spread_gates(b0):
            bank = psum.tile([P, 4, P], F32, name="bank", tag="two")
            for b in range(4):
                nc.tensor.transpose(bank[:, b, :], gate_cols[:, b0 + b : b0 + b + 1].to_broadcast([P, P]), ident[:])
            dst = gates[:, :, b0 * GATE_RUN : (b0 + 4) * GATE_RUN].rearrange("p r (b i) -> p b r i", b=4)
            src = bank[:, :, 0 : TOP * GATE_RUN].rearrange("p b (r i) -> p b r i", r=TOP)
            nc.scalar.copy(out=dst, in_=src)

        for b0 in range(0, GATE_EARLY, 4):
            spread_gates(b0)

        h_words = []
        h_scales = []

        def second_weights(half, first, count, packed):
            for i in range(count):
                cast_interleave((half, first + i) in W2_ON_VECTOR, packed[:, i, :, :], w2_raw[first + i][:, :, half * P : (half + 1) * P])
            words = ring.tile([P, count * P], U32, name="w2_words", align_bytes=64)
            scales = ring.tile([P, count * P], U8, name="w2_scales", align_bytes=64)
            quantize(words[:], scales[:], packed.rearrange("p e n j -> p (e n j)"))
            return words, scales

        def acc_tag(half, e0):
            if half == 0:
                return f"acc{e0 // (2 - (e0 >= E - 2)) % 2}"
            return ("acc0", "acc1", "bank2", "bank3")[e0 // 2]

        def second_layer(half, first, count, words, scales):
            step = 1 if (half, first + count) == (0, E) else 2
            for i0 in range(0, count, step):
                acc = psum.tile([P, step, C], F32, name="acc", tag=acc_tag(half, first + i0), bufs=1)
                for i in range(i0, i0 + step):
                    nc.tensor.matmul_mx(
                        out=acc[:, i - i0, :],
                        lhsT=words[:, i * P : (i + 1) * P].bitcast(FP8X4),
                        lhsT_scale=scales[:, i * P : (i + 1) * P],
                        rhs=h_words[first + i][:].bitcast(FP8X4),
                        rhs_scale=h_scales[first + i][:],
                        start=True,
                        stop=True,
                    )
                e0 = first + i0
                dst = y[half][:, e0 * C : (e0 + step) * C]
                if half == 0 and e0 in Y_ON_VECTOR:
                    nc.vector.tensor_copy(out=dst, in_=acc[:].rearrange("p e s -> p (e s)"))
                else:
                    nc.scalar.copy(out=dst, in_=acc[:].rearrange("p e s -> p (e s)"))

        spent = [raw[:].rearrange("p j i -> p (j i)").bitcast(BF16) for raw in w1_raw]

        gathered = []

        def prepare(e):
            if e in GATHERS:
                count = GATHERS[e] * C
                tag = f"stage{(e - 1) % W1_SLOTS}" if e >= 2 else f"first{e}"
                slot_words = keep.tile([P, count], U32, name="slot_words", tag=tag, align_bytes=64)
                entries = offs_sb[:, e * C // LIST_COL : (e * C + count) // LIST_COL]
                nc.vector.tensor_copy(out=slot_words[:], in_=x_words[:].indirect(entries))
            if e in SCALE_GATHERS:
                count = SCALE_GATHERS[e] * C
                some_scales = ring.tile([P, count], U8, name="slot_scales", bufs=2, align_bytes=64)
                entries = offs_sb[:, e * C // LIST_COL : (e * C + count) // LIST_COL]
                nc.vector.tensor_copy(out=some_scales[:], in_=x_scales[:].indirect(entries))
                for i in range(SCALE_GATHERS[e]):
                    gathered.append(some_scales[:, i * C : (i + 1) * C])
            slot_scales = gathered[e]
            packed = keep.tile([P, PACK, P, PACK], BF16, name="w1_packed", tag=f"stage{e % W1_SLOTS}", align_bytes=64)
            for t0, t1, on_vector in W1_CUTS[e]:
                cast(
                    on_vector,
                    packed[:, t0:t1, :, :].rearrange("p t m j -> p m j t"),
                    w1_raw[e][:].rearrange("p j (m t) -> p m j t", t=PACK)[:, :, :, t0:t1],
                )
            w_words = ring.tile([P, H], U32, name="w1_words", bufs=2, align_bytes=64)
            w_scales = ring.tile([P, H], U8, name="w1_scales", bufs=2, align_bytes=64)
            quantize(w_words[:], w_scales[:], packed[:].rearrange("p t m j -> p (t m j)"))
            return slot_words, slot_scales, w_words, w_scales

        def first_layer(e, slot_words, slot_scales, w_words, w_scales):
            h_flat = spent[min(e + 1, E - 1)][:, (e % 4) * C * PACK : (e % 4 + 1) * C * PACK]
            h_packed = h_flat.rearrange("p (s t) -> p s t", t=PACK)
            for s0 in range(0, C, P):
                a = psum.tile([P, PACK, P], F32, name="a", tag=f"bank{(2 * e + s0 // P) % 4}", bufs=1)
                for t in range(PACK):
                    cols = slice(t * P, (t + 1) * P)
                    nc.tensor.matmul_mx(
                        out=a[:, t, :],
                        lhsT=w_words[:, cols].bitcast(FP8X4),
                        lhsT_scale=w_scales[:, cols],
                        rhs=slot_words[:, s0 : s0 + P].bitcast(FP8X4),
                        rhs_scale=slot_scales[:, s0 : s0 + P],
                        start=True,
                        stop=True,
                    )
                nc.scalar.activation(out=h_packed[:, s0 : s0 + P, :], in_=a[:].rearrange("p t s -> p s t"), func=SILU)
            words = keep.tile([P, C], U32, name=f"h_words{e}", align_bytes=64)
            scales = keep.tile([P, C], U8, name=f"h_scales{e}", align_bytes=64)
            quantize(words[:], scales[:], h_flat)
            h_words.append(words)
            h_scales.append(scales)

        ready = [prepare(e) for e in range(AHEAD)]
        for e in range(E + SECOND_LAG):
            if e + AHEAD < E:
                ready.append(prepare(e + AHEAD))
            if e < E:
                first_layer(e, *ready[e])
            if e >= SECOND_LAG and (e - SECOND_LAG) % 2 == 1:
                w2_packed = ring.tile([P, 2, P, PACK], BF16, name="w2_packed", align_bytes=64)
                first = e - SECOND_LAG - 1
                second_layer(0, first, 2, *second_weights(0, first, 2, w2_packed[:]))

        totals = []

        def combine(half, c0, width, last, given=()):
            products = []
            for r in range(TOP):
                if r < len(given):
                    product = given[r]
                else:
                    product = ring.tile([P, width], F32, name=f"product{r}")[:]
                entries = pos_sb[r][:, c0 // LIST_COL : (c0 + width) // LIST_COL]
                nc.vector.tensor_tensor(product, y[half][:].indirect(entries), gates[:, r, c0 : c0 + width], MULT)
                products.append(product)
            result = ring.tile([P, width], F32, name="result", bufs=4)
            if last:
                partial = ring.tile([P, width], F32, name="summed")
                nc.vector.tensor_tensor(partial[:], products[0], products[1], ADD)
                nc.vector.tensor_tensor(result[:], partial[:], products[2], ADD)
            else:
                total = psum.tile([P, BANK], F32, name="total", tag=f"bank{len(totals) % 2}", bufs=1)
                totals.append(total)
                for b0 in range(0, width, P):
                    for r in range(TOP):
                        nc.tensor.matmul(
                            total[:, b0 : b0 + P],
                            lhsT=products[r][:, b0 : b0 + P],
                            rhs=ident[:],
                            start=(r == 0),
                            stop=(r == TOP - 1),
                            is_transpose=True,
                        )
                summed = ring.tile([P, width], F32, name="summed")
                nc.scalar.copy(out=summed[:], in_=total[:, 0:width])
                back = psum.tile([P, BANK], F32, name="back", tag="two")
                for b0 in range(0, width, P):
                    nc.tensor.transpose(back[:, b0 : b0 + P], summed[:, b0 : b0 + P], ident[:])
                nc.scalar.copy(out=result[:], in_=back[:, 0:width])
            nc.sync.dma_start(out=out[half * P : (half + 1) * P, c0 : c0 + width], in_=result[:])

        for b0 in range(GATE_EARLY, GATE_ROWS, 4):
            spread_gates(b0)
        late = spent[E - 1]
        upper = second_weights(1, 0, E, late.rearrange("p (e n j) -> p e n j", n=P, j=PACK))
        combine(0, 0, 384, False)
        second_layer(1, 0, E, *upper)
        combine(0, 384, 512, False, [late.bitcast(F32)[:, r * 512 : (r + 1) * 512] for r in range(TOP)])
        combine(0, 384 + 512, 768 - 384, False, [late.bitcast(F32)[:, 1536 : 1536 + 768 - 384]])
        for c0, width in LAST_CHUNKS:
            combine(1, c0, width, c0 >= 1024)
